import numpy as np
import ml_dtypes


def mxq(x, axis, fmt="e4m3"):
    dtype, down = {"e4m3": (ml_dtypes.float8_e4m3fn, 7), "e5m2": (ml_dtypes.float8_e5m2, 14)}[fmt]
    v = np.moveaxis(np.asarray(x, np.float32).astype(ml_dtypes.bfloat16).astype(np.float64), axis, -1)
    blocks = v.reshape(v.shape[:-1] + (-1, 32))
    amax = np.abs(blocks).max(-1, keepdims=True)
    byte = np.maximum(np.where(amax > 0, np.frexp(amax)[1] - 1 + 127, 0) - down, 1)
    scale = np.exp2(byte - 127.0)
    codes = (blocks / scale).astype(np.float32).astype(dtype).astype(np.float64)
    return np.moveaxis((codes * scale).reshape(v.shape), -1, axis)


WIDE = False


def mx_kscale(k):
    if not WIDE:
        return np.ones(k)
    levels = np.array([30, -30])
    if k % 512:
        return np.exp2(np.random.permutation(np.resize(levels, k // 32))).repeat(32)
    a = np.empty((k // 512, 16))
    for p in range(k // 512):
        a[p, :8] = np.random.permutation(np.resize(levels, 8))
        for g in range(8):
            far = levels[np.abs(levels - a[p, g]) >= 10]
            a[p, g + 8] = far[np.random.randint(len(far))]
    return np.exp2(a.ravel()).repeat(32)


def f64(x):
    return np.asarray(x).astype(np.float64)


def striped(idx):
    return np.tile(np.asarray(idx).reshape(-1, 16).T, (8, 1)).astype(np.uint16)


def unstriped(offs):
    return offs[:16].T.reshape(-1).astype(np.int64)


E2M1 = np.array([0.0, 0.5, 1.0, 1.5, 2.0, 3.0, 4.0, 6.0, -0.0, -0.5, -1.0, -1.5, -2.0, -3.0, -4.0, -6.0])


def pack_weight(w, fmt):
    k, n = w.shape
    w = f64(np.asarray(w, np.float32).astype(ml_dtypes.bfloat16)).reshape(k // 32, 32, n)
    amax = np.abs(w).max(1)
    if fmt in ("e4m3", "e5m2"):
        byte = np.frexp(amax)[1] - 1 + 127 - (7 if fmt == "e4m3" else 14)
    else:
        mant, ex = np.frexp(amax / 6.0)
        byte = np.where(mant > 0.5, ex, ex - 1) + 127
    byte = np.clip(np.where(amax > 0, byte, 1), 1, 254)
    scaled = (w * np.exp2(127.0 - byte)[:, None, :]).reshape(k, n).astype(np.float32)
    by_word = np.ascontiguousarray(scaled.reshape(k // 512, 128, 4, n).transpose(0, 1, 3, 2))
    if fmt in ("e4m3", "e5m2"):
        words = by_word.astype(ml_dtypes.float8_e4m3fn if fmt == "e4m3" else ml_dtypes.float8_e5m2).view(np.uint8)
    else:
        c = by_word.astype(ml_dtypes.float4_e2m1fn).view(np.uint8) & 0xF
        words = (c[..., 0::2] | (c[..., 1::2] << 4)).reshape(k // 512, 128, 2 * n)
    return np.ascontiguousarray(words), np.ascontiguousarray(byte.astype(np.uint8).reshape(k // 512, 16, n))


def unpack_weight(words, scales, fmt):
    g, _, n = scales.shape
    words = np.ascontiguousarray(words).reshape(g, 128, n, -1)
    if fmt in ("e4m3", "e5m2"):
        vals = words.view(ml_dtypes.float8_e4m3fn if fmt == "e4m3" else ml_dtypes.float8_e5m2).astype(np.float64)
    else:
        nib = np.empty((g, 128, n, 4), np.uint8)
        nib[..., 0::2] = words & 0xF
        nib[..., 1::2] = words >> 4
        vals = E2M1[nib]
    vals = vals * np.repeat(np.exp2(scales.astype(np.float64) - 127.0), 8, axis=1)[..., None]
    return vals.transpose(0, 1, 3, 2).reshape(g * 512, n)


K, T, Z, J, R, C, N, L, E = 512, 1024, 1024, 256, 512, 512, 256, 512, 128


def setup_inputs():
    n = np.random.standard_normal
    idx = np.random.permutation(T)[:J]
    idx2 = np.random.permutation(Z)[:J]
    idx3 = np.random.permutation(C)[:J]
    idx4 = np.random.permutation(C)[:J]
    idx5 = np.random.permutation(J)[:E]
    idx6 = np.random.permutation(J)[:E]
    fk = mx_kscale(K)
    fr = mx_kscale(R)
    fl = mx_kscale(L)
    xtp = pack_weight(n((K, T)) / fk[:, None], "e2m1")
    xop = pack_weight(n((K, Z)) / fk[:, None], "e4m3")
    wp = pack_weight(n((K, R)) * 1 / np.sqrt(K) * fk[:, None] * fr, "e4m3")
    w2p = pack_weight(n((K, R)) * 1 / np.sqrt(K) * fk[:, None] * fr, "e5m2")
    wbp = pack_weight(n((R, N)) * 1 / np.sqrt(R) / fr[:, None], "e2m1")
    sxp = pack_weight(n((L, J)) / fl[:, None], "e4m3")
    wsp = pack_weight(n((L, N)) * 1 / np.sqrt(L) * fl[:, None], "e4m3")
    return {
        "xt_words": xtp[0],
        "xt_scales": xtp[1],
        "xo_words": xop[0],
        "xo_scales": xop[1],
        "w_words": wp[0],
        "w_scales": wp[1],
        "w2_words": w2p[0],
        "w2_scales": w2p[1],
        "wb_words": wbp[0],
        "wb_scales": wbp[1],
        "sx_words": sxp[0],
        "sx_scales": sxp[1],
        "ws_words": wsp[0],
        "ws_scales": wsp[1],
        "offs": striped(idx),
        "offs2": striped(idx2),
        "offs3": striped(idx3),
        "offs4": striped(idx4),
        "offs5": striped(idx5),
        "offs6": striped(idx6),
    }


def reference(xt_words, xt_scales, xo_words, xo_scales, w_words, w_scales, w2_words, w2_scales, wb_words, wb_scales, sx_words, sx_scales, ws_words, ws_scales, offs, offs2, offs3, offs4, offs5, offs6):
    idx = unstriped(offs)
    idx2 = unstriped(offs2)
    idx3 = unstriped(offs3)
    idx4 = unstriped(offs4)
    idx5 = unstriped(offs5)
    idx6 = unstriped(offs6)
    xtu = unpack_weight(xt_words, xt_scales, "e2m1")
    xou = unpack_weight(xo_words, xo_scales, "e4m3")
    wu = unpack_weight(w_words, w_scales, "e4m3")
    w2u = unpack_weight(w2_words, w2_scales, "e5m2")
    wbu = unpack_weight(wb_words, wb_scales, "e2m1")
    sxu = unpack_weight(sx_words, sx_scales, "e4m3")
    wsu = unpack_weight(ws_words, ws_scales, "e4m3")
    xtidxg = xtu[:, idx]
    xoidx2g = xou[:, idx2]
    a = wu.T @ xtidxg + w2u.T @ xoidx2g
    b = w2u.T @ xtidxg + wu.T @ xoidx2g
    pw = np.zeros((R, C))
    pw[:, idx3] = a
    hid = np.maximum(pw[:, idx4], b)
    hidq = mxq(hid, 0, "e5m2")
    p = wbu.T @ hidq + wsu.T @ sxu
    y = np.maximum(p[:, idx5], p[:, idx6])
    return y

@@ -1,0 +1,193 @@
+from contextlib import ExitStack
+
+import concourse.mybir as mybir
+
+F32 = mybir.dt.float32
+BF16 = mybir.dt.bfloat16
+I32 = mybir.dt.int32
+U32 = mybir.dt.uint32
+U16 = mybir.dt.uint16
+U8 = mybir.dt.uint8
+E4M3 = mybir.dt.float8_e4m3fn_x4
+E5M2 = mybir.dt.float8_e5m2_x4
+E2M1 = mybir.dt.float4_e2m1fn_x4
+COPY = mybir.ActivationFunctionType.Copy
+MAX = mybir.AluOpType.max
+
+P = 128
+T, Z, J, R, C, N, E = 1024, 1024, 256, 512, 512, 256, 128
+PACK = 4
+ROWS = 16
+TOP = P - ROWS
+
+FLOPS = 2 * 512 * (4 * R * J + 2 * N * J)
+
+
+def tile_list_crossed_board_skip_bestoftwo_kernel(
+    tc, xt_words, xt_scales, xo_words, xo_scales, w_words, w_scales, w2_words, w2_scales,
+    wb_words, wb_scales, sx_words, sx_scales, ws_words, ws_scales,
+    offs, offs2, offs3, offs4, offs5, offs6, out,
+):
+    nc = tc.nc
+    with ExitStack() as ctx:
+        sb = ctx.enter_context(tc.tile_pool(name="sb", bufs=1))
+        ps = ctx.enter_context(tc.psum_pool(name="ps", bufs=1))
+
+        def tile(name, shape, dtype):
+            return sb.tile(shape, dtype, name=name, align_bytes=64)
+
+        def words32(dram):
+            return dram[0].rearrange("p n t -> p (n t)").bitcast(I32)
+
+        lists = {}
+        for name, n in (("o1", J), ("o2", J), ("o3", J), ("o4", J), ("o5", E), ("o6", E)):
+            lists[name] = tile(name, [P, n // 16], U16)
+
+        xt_w = tile("xt_w", [P, T], U16)
+        xo_w = tile("xo_w", [P, Z], U32)
+        xt_s = tile("xt_s", [P, T], U8)
+        xo_s = tile("xo_s", [P, Z], U8)
+        w_raw = tile("w_raw", [P, R], U32)
+        w2_raw = tile("w2_raw", [P, R], U32)
+        wsc_raw = tile("wsc_raw", [P, 2, R], U8)
+        wb_w = tile("wb_w", [P, 2 * N], U8)
+        sx_w = tile("sx_w", [P, J], U32)
+        ws_w = tile("ws_w", [P, N], U32)
+        planes = tile("planes", [P, 2 * J + 2 * R + 3 * N], U8)
+        LATE = 2 * J + 2 * R
+
+        nc.sync.dma_start(lists["o1"][:], offs)
+        nc.sync.dma_start(out=xt_s[TOP:P, :].bitcast(I32), in_=xt_scales[0].bitcast(I32))
+        nc.sync.dma_start(lists["o2"][:], offs2)
+        nc.sync.dma_start(out=xo_s[TOP:P, :].bitcast(I32), in_=xo_scales[0].bitcast(I32))
+        nc.sync.dma_start(out=wsc_raw[TOP:P, 0, :].bitcast(I32), in_=w_scales[0].bitcast(I32))
+        nc.sync.dma_start(out=wsc_raw[TOP:P, 1, :].bitcast(I32), in_=w2_scales[0].bitcast(I32))
+        nc.sync.dma_start(out=xt_w[:].bitcast(I32), in_=xt_words[0].bitcast(I32))
+        nc.sync.dma_start(out=xo_w[:].bitcast(I32), in_=words32(xo_words))
+        for i, scales in enumerate((wb_scales, sx_scales, ws_scales)):
+            nc.sync.dma_start(
+                out=planes[TOP:P, LATE + N * i : LATE + N * (i + 1)].bitcast(I32), in_=scales[0].bitcast(I32)
+            )
+        nc.gpsimd.dma_start(out=w_raw[:].bitcast(I32), in_=words32(w_words))
+        nc.gpsimd.dma_start(out=w2_raw[:].bitcast(I32), in_=words32(w2_words))
+        nc.sync.dma_start(lists["o3"][:], offs3)
+        nc.sync.dma_start(lists["o4"][:], offs4)
+        nc.sync.dma_start(lists["o5"][:], offs5)
+        nc.sync.dma_start(lists["o6"][:], offs6)
+        nc.gpsimd.dma_start(out=sx_w[:].bitcast(I32), in_=words32(sx_words))
+        nc.gpsimd.dma_start(out=ws_w[:].bitcast(I32), in_=words32(ws_words))
+        nc.gpsimd.dma_start(out=wb_w[:].bitcast(I32), in_=wb_words[0].bitcast(I32))
+
+        nc.vector.memset(xt_s[0:TOP, :].bitcast(I32), 0)
+        nc.vector.memset(xo_s[0:TOP, :].bitcast(I32), 0)
+        nc.vector.memset(wsc_raw[0:TOP, :, :].rearrange("p g r -> p (g r)").bitcast(I32), 0)
+        nc.vector.memset(planes[0:TOP, LATE:].bitcast(I32), 0)
+        boards = [tile("board%d" % t, [P, C], F32) for t in range(PACK)]
+        for t in range(PACK):
+            nc.vector.memset(boards[t][:], 0.0)
+
+        xt_gs = tile("xt_gs", [P, J], U8)
+        xo_gs = tile("xo_gs", [P, J], U8)
+        nc.vector.tensor_copy(xt_gs[:], xt_s[:].indirect(lists["o1"][:]))
+        nc.vector.tensor_copy(xo_gs[:], xo_s[:].indirect(lists["o2"][:]))
+        nc.vector.tensor_copy(
+            out=planes[:, 2 * J : LATE].rearrange("p (g t m) -> p g t m", g=2, t=PACK),
+            in_=wsc_raw[:].rearrange("p g (m t) -> p g t m", t=PACK),
+        )
+        nc.vector.tensor_copy(out=planes[:, 0:J].bitcast(I32), in_=xt_gs[:].bitcast(I32))
+        nc.vector.tensor_copy(out=planes[:, J : 2 * J].bitcast(I32), in_=xo_gs[:].bitcast(I32))
+        for q in range(4):
+            nc.sync.dma_start(
+                out=planes[32 * q : 32 * q + 4, :].bitcast(I32),
+                in_=planes[TOP + 4 * q : TOP + 4 * q + 4, :].bitcast(I32),
+            )
+
+        xt_g = tile("xt_g", [P, J], U16)
+        xo_g = tile("xo_g", [P, J], U32)
+        nc.vector.tensor_copy(xt_g[:], xt_w[:].indirect(lists["o1"][:]))
+        nc.vector.tensor_copy(xo_g[:], xo_w[:].indirect(lists["o2"][:]))
+        w_p = tile("w_p", [P, R], U32)
+        w2_p = tile("w2_p", [P, R], U32)
+        for dealt, raw in ((w_p, w_raw), (w2_p, w2_raw)):
+            nc.scalar.copy(
+                out=dealt[:].rearrange("p (t m) -> p m t", t=PACK),
+                in_=raw[:].rearrange("p (m t) -> p m t", t=PACK),
+            )
+
+        xt_op = (xt_g[:].bitcast(E2M1), planes[:, 0:J])
+        xo_op = (xo_g[:].bitcast(E4M3), planes[:, J : 2 * J])
+
+        def w_op(t):
+            return (w_p[:, P * t : P * (t + 1)].bitcast(E4M3), planes[:, 2 * J + P * t : 2 * J + P * (t + 1)])
+
+        def w2_op(t):
+            base = 2 * J + R
+            return (w2_p[:, P * t : P * (t + 1)].bitcast(E5M2), planes[:, base + P * t : base + P * (t + 1)])
+
+        def mx(dst, still, moving, start, stop):
+            nc.tensor.matmul_mx(
+                out=dst, lhsT=still[0], lhsT_scale=still[1], rhs=moving[0], rhs_scale=moving[1], start=start, stop=stop
+            )
+
+        a_ps = [ps.tile([P, J], F32, name="a_ps%d" % t) for t in range(PACK)]
+        b_ps = [ps.tile([P, 2, J], F32, name="b_ps%d" % u) for u in range(2)]
+        p_ps = [ps.tile([P, J], F32, name="p_ps%d" % h) for h in range(2)]
+        for t in (0, 2, 1, 3):
+            mx(a_ps[t][:], w_op(t), xt_op, True, False)
+            mx(a_ps[t][:], w2_op(t), xo_op, False, True)
+        for t in range(PACK):
+            mx(b_ps[t // 2][:, t % 2, :], w2_op(t), xt_op, True, False)
+            mx(b_ps[t // 2][:, t % 2, :], w_op(t), xo_op, False, True)
+        for h in range(2):
+            mx(
+                p_ps[h][:],
+                (ws_w[:, P * h : P * (h + 1)].bitcast(E4M3), planes[:, LATE + 2 * N + P * h : LATE + 2 * N + P * (h + 1)]),
+                (sx_w[:].bitcast(E4M3), planes[:, LATE + N : LATE + 2 * N]),
+                True,
+                False,
+            )
+
+        a_sb = [tile("a_sb%d" % t, [P, J], F32) for t in range(PACK)]
+        read = [tile("read%d" % u, [P, 2, J], F32) for u in range(2)]
+        for t in (0, 1):
+            nc.vector.tensor_copy(out=a_sb[t][:], in_=a_ps[t][:])
+            nc.vector.tensor_copy(boards[t][:].indirect(lists["o3"][:]), a_sb[t][:])
+        for t in (0, 1):
+            nc.vector.tensor_copy(read[0][:, t, :], boards[t][:].indirect(lists["o4"][:]))
+        for t in (2, 3):
+            nc.scalar.copy(out=a_sb[t][:], in_=a_ps[t][:])
+            nc.scalar.activation(boards[t][:].indirect(lists["o3"][:]), a_sb[t][:], COPY)
+        for t in (2, 3):
+            nc.scalar.activation(read[1][:, t - 2, :], boards[t][:].indirect(lists["o4"][:]), COPY)
+
+        hid = tile("hid", [P, J, PACK], BF16)
+        for u in range(2):
+            nc.vector.tensor_tensor(
+                out=hid[:, :, 2 * u : 2 * u + 2],
+                in0=read[u][:].rearrange("p t j -> p j t"),
+                in1=b_ps[u][:].rearrange("p t j -> p j t"),
+                op=MAX,
+            )
+        hid_w = tile("hid_w", [P, J], U32)
+        hid_s = tile("hid_s", [P, J], U8)
+        nc.vector.quantize_mx(out=hid_w[:].bitcast(E5M2), scales=hid_s[:], in_=hid[:].rearrange("p j t -> p (j t)"))
+        for h in range(2):
+            mx(
+                p_ps[h][:],
+                (wb_w[:, 2 * P * h : 2 * P * (h + 1)].bitcast(E2M1), planes[:, LATE + P * h : LATE + P * (h + 1)]),
+                (hid_w[:].bitcast(E5M2), hid_s[:]),
+                False,
+                True,
+            )
+
+        p_sb = [tile("p_sb%d" % h, [P, J], F32) for h in range(2)]
+        pick = [[tile("pick%d_%d" % (h, i), [P, E], F32) for i in range(2)] for h in range(2)]
+        best = [tile("best%d" % h, [P, E], F32) for h in range(2)]
+        nc.vector.tensor_copy(out=p_sb[0][:], in_=p_ps[0][:])
+        nc.scalar.copy(out=p_sb[1][:], in_=p_ps[1][:])
+        for i, name in enumerate(("o5", "o6")):
+            nc.vector.tensor_copy(pick[0][i][:], p_sb[0][:].indirect(lists[name][:]))
+            nc.scalar.activation(pick[1][i][:], p_sb[1][:].indirect(lists[name][:]), COPY)
+        for h in range(2):
+            nc.vector.tensor_tensor(out=best[h][:], in0=pick[h][0][:], in1=pick[h][1][:], op=MAX)
+            nc.sync.dma_start(out=out[P * h : P * (h + 1), :], in_=best[h][:])

@@ -31,6 +31,7 @@ def tile_list_crossed_board_skip_bestoftwo_kernel(
     nc = tc.nc
     with ExitStack() as ctx:
         sb = ctx.enter_context(tc.tile_pool(name="sb", bufs=1))
+        early = ctx.enter_context(tc.tile_pool(name="early", bufs=1))
         ps = ctx.enter_context(tc.psum_pool(name="ps", bufs=1))
 
         def tile(name, shape, dtype):
@@ -44,46 +45,36 @@ def tile_list_crossed_board_skip_bestoftwo_kernel(
             lists[name] = tile(name, [P, n // 16], U16)
 
         xt_w = tile("xt_w", [P, T], U16)
-        xo_w = tile("xo_w", [P, Z], U32)
+        xo_w = early.tile([P, Z], U32, name="xo_w", offset=0, align_bytes=64)
         xt_s = tile("xt_s", [P, T], U8)
         xo_s = tile("xo_s", [P, Z], U8)
-        w_raw = tile("w_raw", [P, R], U32)
-        w2_raw = tile("w2_raw", [P, R], U32)
-        wsc_raw = tile("wsc_raw", [P, 2, R], U8)
-        wb_w = tile("wb_w", [P, 2 * N], U8)
-        sx_w = tile("sx_w", [P, J], U32)
-        ws_w = tile("ws_w", [P, N], U32)
-        planes = tile("planes", [P, 2 * J + 2 * R + 3 * N], U8)
+        w_raw = sb.tile([P, R], U32, name="w_raw", tag="raw_a", align_bytes=64)
+        w2_raw = sb.tile([P, R], U32, name="w2_raw", tag="raw_b", align_bytes=64)
+        wsc_raw = sb.tile([P, 2, R], U8, name="wsc_raw", tag="raw_c", align_bytes=64)
         LATE = 2 * J + 2 * R
+        stage = tile("stage", [P, LATE], U8)
+        planes = tile("planes", [P, LATE + 3 * N], U8)
 
         nc.sync.dma_start(lists["o1"][:], offs)
-        nc.sync.dma_start(out=xt_s[TOP:P, :].bitcast(I32), in_=xt_scales[0].bitcast(I32))
+        nc.scalar.dma_start(out=xt_s[TOP:P, :].bitcast(I32), in_=xt_scales[0].bitcast(I32))
         nc.sync.dma_start(lists["o2"][:], offs2)
-        nc.sync.dma_start(out=xo_s[TOP:P, :].bitcast(I32), in_=xo_scales[0].bitcast(I32))
-        nc.sync.dma_start(out=wsc_raw[TOP:P, 0, :].bitcast(I32), in_=w_scales[0].bitcast(I32))
-        nc.sync.dma_start(out=wsc_raw[TOP:P, 1, :].bitcast(I32), in_=w2_scales[0].bitcast(I32))
-        nc.sync.dma_start(out=xt_w[:].bitcast(I32), in_=xt_words[0].bitcast(I32))
+        nc.scalar.dma_start(out=xo_s[TOP:P, :].bitcast(I32), in_=xo_scales[0].bitcast(I32))
         nc.sync.dma_start(out=xo_w[:].bitcast(I32), in_=words32(xo_words))
-        for i, scales in enumerate((wb_scales, sx_scales, ws_scales)):
-            nc.sync.dma_start(
-                out=planes[TOP:P, LATE + N * i : LATE + N * (i + 1)].bitcast(I32), in_=scales[0].bitcast(I32)
-            )
-        nc.gpsimd.dma_start(out=w_raw[:].bitcast(I32), in_=words32(w_words))
-        nc.gpsimd.dma_start(out=w2_raw[:].bitcast(I32), in_=words32(w2_words))
+        nc.scalar.dma_start(out=wsc_raw[TOP:P, 0, :].bitcast(I32), in_=w_scales[0].bitcast(I32))
+        nc.sync.dma_start(out=w_raw[:].bitcast(I32), in_=words32(w_words))
+        nc.scalar.dma_start(out=wsc_raw[TOP:P, 1, :].bitcast(I32), in_=w2_scales[0].bitcast(I32))
+        nc.sync.dma_start(out=w2_raw[:].bitcast(I32), in_=words32(w2_words))
+        nc.sync.dma_start(out=xt_w[:].bitcast(I32), in_=xt_words[0].bitcast(I32))
         nc.sync.dma_start(lists["o3"][:], offs3)
         nc.sync.dma_start(lists["o4"][:], offs4)
         nc.sync.dma_start(lists["o5"][:], offs5)
         nc.sync.dma_start(lists["o6"][:], offs6)
-        nc.gpsimd.dma_start(out=sx_w[:].bitcast(I32), in_=words32(sx_words))
-        nc.gpsimd.dma_start(out=ws_w[:].bitcast(I32), in_=words32(ws_words))
-        nc.gpsimd.dma_start(out=wb_w[:].bitcast(I32), in_=wb_words[0].bitcast(I32))
 
         nc.vector.memset(xt_s[0:TOP, :].bitcast(I32), 0)
         nc.vector.memset(xo_s[0:TOP, :].bitcast(I32), 0)
         nc.vector.memset(wsc_raw[0:TOP, :, :].rearrange("p g r -> p (g r)").bitcast(I32), 0)
-        nc.vector.memset(planes[0:TOP, LATE:].bitcast(I32), 0)
-        boards = [tile("board%d" % t, [P, C], F32) for t in range(PACK)]
-        for t in range(PACK):
+        boards = {t: tile("board%d" % t, [P, C], F32) for t in (0, 2)}
+        for t in (0, 2):
             nc.vector.memset(boards[t][:], 0.0)
 
         xt_gs = tile("xt_gs", [P, J], U8)
@@ -91,21 +82,31 @@ def tile_list_crossed_board_skip_bestoftwo_kernel(
         nc.vector.tensor_copy(xt_gs[:], xt_s[:].indirect(lists["o1"][:]))
         nc.vector.tensor_copy(xo_gs[:], xo_s[:].indirect(lists["o2"][:]))
         nc.vector.tensor_copy(
-            out=planes[:, 2 * J : LATE].rearrange("p (g t m) -> p g t m", g=2, t=PACK),
+            out=stage[:, 2 * J : LATE].rearrange("p (g t m) -> p g t m", g=2, t=PACK),
             in_=wsc_raw[:].rearrange("p g (m t) -> p g t m", t=PACK),
         )
-        nc.vector.tensor_copy(out=planes[:, 0:J].bitcast(I32), in_=xt_gs[:].bitcast(I32))
-        nc.vector.tensor_copy(out=planes[:, J : 2 * J].bitcast(I32), in_=xo_gs[:].bitcast(I32))
-        for q in range(4):
-            nc.sync.dma_start(
-                out=planes[32 * q : 32 * q + 4, :].bitcast(I32),
-                in_=planes[TOP + 4 * q : TOP + 4 * q + 4, :].bitcast(I32),
-            )
+        nc.vector.tensor_copy(out=stage[:, 0:J].bitcast(I32), in_=xt_gs[:].bitcast(I32))
+        nc.vector.tensor_copy(out=stage[:, J : 2 * J].bitcast(I32), in_=xo_gs[:].bitcast(I32))
+
+        def spread(first, width):
+            for q in range(4):
+                nc.sync.dma_start(
+                    out=planes[32 * q : 32 * q + 4, first : first + width].bitcast(I32),
+                    in_=stage[TOP + 4 * q : TOP + 4 * q + 4, 0:width].bitcast(I32),
+                )
+
+        spread(0, LATE)
+        for i, scales in enumerate((wb_scales, sx_scales, ws_scales)):
+            nc.sync.dma_start(out=stage[TOP:P, N * i : N * (i + 1)].bitcast(I32), in_=scales[0].bitcast(I32))
+        spread(LATE, 3 * N)
 
         xt_g = tile("xt_g", [P, J], U16)
         xo_g = tile("xo_g", [P, J], U32)
-        nc.vector.tensor_copy(xt_g[:], xt_w[:].indirect(lists["o1"][:]))
         nc.vector.tensor_copy(xo_g[:], xo_w[:].indirect(lists["o2"][:]))
+        nc.vector.tensor_copy(xt_g[:], xt_w[:].indirect(lists["o1"][:]))
+        for t in (1, 3):
+            boards[t] = early.tile([P, C], F32, name="board%d" % t, offset=4 * C * (t // 2), align_bytes=64)
+            nc.vector.memset(boards[t][:], 0.0)
         w_p = tile("w_p", [P, R], U32)
         w2_p = tile("w2_p", [P, R], U32)
         for dealt, raw in ((w_p, w_raw), (w2_p, w2_raw)):
@@ -113,6 +114,13 @@ def tile_list_crossed_board_skip_bestoftwo_kernel(
                 out=dealt[:].rearrange("p (t m) -> p m t", t=PACK),
                 in_=raw[:].rearrange("p (m t) -> p m t", t=PACK),
             )
+
+        sx_w = sb.tile([P, J], U32, name="sx_w", tag="raw_a", align_bytes=64)
+        ws_w = sb.tile([P, N], U32, name="ws_w", tag="raw_b", align_bytes=64)
+        wb_w = sb.tile([P, 2 * N], U8, name="wb_w", tag="raw_c", align_bytes=64)
+        nc.gpsimd.dma_start(out=sx_w[:].bitcast(I32), in_=words32(sx_words))
+        nc.gpsimd.dma_start(out=ws_w[:].bitcast(I32), in_=words32(ws_words))
+        nc.gpsimd.dma_start(out=wb_w[:].bitcast(I32), in_=wb_words[0].bitcast(I32))
 
         xt_op = (xt_g[:].bitcast(E2M1), planes[:, 0:J])
         xo_op = (xo_g[:].bitcast(E4M3), planes[:, J : 2 * J])
@@ -129,12 +137,30 @@ def tile_list_crossed_board_skip_bestoftwo_kernel(
                 out=dst, lhsT=still[0], lhsT_scale=still[1], rhs=moving[0], rhs_scale=moving[1], start=start, stop=stop
             )
 
+        a_sb = [tile("a_sb%d" % t, [P, J], F32) for t in range(PACK)]
         a_ps = [ps.tile([P, J], F32, name="a_ps%d" % t) for t in range(PACK)]
         b_ps = [ps.tile([P, 2, J], F32, name="b_ps%d" % u) for u in range(2)]
         p_ps = [ps.tile([P, J], F32, name="p_ps%d" % h) for h in range(2)]
-        for t in (0, 2, 1, 3):
-            mx(a_ps[t][:], w_op(t), xt_op, True, False)
-            mx(a_ps[t][:], w2_op(t), xo_op, False, True)
+        H = J // 2
+
+        def cols(op, lo, hi):
+            return (op[0][:, lo:hi], op[1][:, lo:hi])
+
+        def place(t, lo, hi):
+            where = boards[t][:].indirect(lists["o3"][:, lo // 16 : hi // 16])
+            if t < 2:
+                nc.vector.tensor_copy(where, a_sb[t][:, lo:hi])
+            else:
+                nc.scalar.activation(where, a_sb[t][:, lo:hi], COPY)
+
+        pieces = ((0, 0, H), (2, 0, H), (0, H, J), (2, H, J), (1, 0, J), (3, 0, J))
+        for i, (t, lo, hi) in enumerate(pieces):
+            mx(a_ps[t][:, lo:hi], w_op(t), cols(xt_op, lo, hi), True, False)
+            mx(a_ps[t][:, lo:hi], w2_op(t), cols(xo_op, lo, hi), False, True)
+            nc.scalar.copy(out=a_sb[t][:, lo:hi], in_=a_ps[t][:, lo:hi])
+            if i > 0:
+                place(*pieces[i - 1])
+        place(*pieces[-1])
         for t in range(PACK):
             mx(b_ps[t // 2][:, t % 2, :], w2_op(t), xt_op, True, False)
             mx(b_ps[t // 2][:, t % 2, :], w_op(t), xo_op, False, True)
@@ -147,38 +173,35 @@ def tile_list_crossed_board_skip_bestoftwo_kernel(
                 False,
             )
 
-        a_sb = [tile("a_sb%d" % t, [P, J], F32) for t in range(PACK)]
         read = [tile("read%d" % u, [P, 2, J], F32) for u in range(2)]
-        for t in (0, 1):
-            nc.vector.tensor_copy(out=a_sb[t][:], in_=a_ps[t][:])
-            nc.vector.tensor_copy(boards[t][:].indirect(lists["o3"][:]), a_sb[t][:])
         for t in (0, 1):
             nc.vector.tensor_copy(read[0][:, t, :], boards[t][:].indirect(lists["o4"][:]))
         for t in (2, 3):
-            nc.scalar.copy(out=a_sb[t][:], in_=a_ps[t][:])
-            nc.scalar.activation(boards[t][:].indirect(lists["o3"][:]), a_sb[t][:], COPY)
-        for t in (2, 3):
             nc.scalar.activation(read[1][:, t - 2, :], boards[t][:].indirect(lists["o4"][:]), COPY)
 
-        hid = tile("hid", [P, J, PACK], BF16)
+        hid = [tile("hid%d" % s, [P, H, PACK], BF16) for s in range(2)]
         for u in range(2):
-            nc.vector.tensor_tensor(
-                out=hid[:, :, 2 * u : 2 * u + 2],
-                in0=read[u][:].rearrange("p t j -> p j t"),
-                in1=b_ps[u][:].rearrange("p t j -> p j t"),
-                op=MAX,
+            for s in range(2):
+                nc.vector.tensor_tensor(
+                    out=hid[s][:, :, 2 * u : 2 * u + 2],
+                    in0=read[u][:, :, H * s : H * (s + 1)].rearrange("p t j -> p j t"),
+                    in1=b_ps[u][:, :, H * s : H * (s + 1)].rearrange("p t j -> p j t"),
+                    op=MAX,
+                )
+        hid_w = [tile("hid_w%d" % s, [P, H], U32) for s in range(2)]
+        hid_s = [tile("hid_s%d" % s, [P, H], U8) for s in range(2)]
+        for s in range(2):
+            nc.vector.quantize_mx(
+                out=hid_w[s][:].bitcast(E5M2), scales=hid_s[s][:], in_=hid[s][:].rearrange("p j t -> p (j t)")
             )
-        hid_w = tile("hid_w", [P, J], U32)
-        hid_s = tile("hid_s", [P, J], U8)
-        nc.vector.quantize_mx(out=hid_w[:].bitcast(E5M2), scales=hid_s[:], in_=hid[:].rearrange("p j t -> p (j t)"))
-        for h in range(2):
-            mx(
-                p_ps[h][:],
-                (wb_w[:, 2 * P * h : 2 * P * (h + 1)].bitcast(E2M1), planes[:, LATE + P * h : LATE + P * (h + 1)]),
-                (hid_w[:].bitcast(E5M2), hid_s[:]),
-                False,
-                True,
-            )
+            for h in range(2):
+                mx(
+                    p_ps[h][:, H * s : H * (s + 1)],
+                    (wb_w[:, 2 * P * h : 2 * P * (h + 1)].bitcast(E2M1), planes[:, LATE + P * h : LATE + P * (h + 1)]),
+                    (hid_w[s][:].bitcast(E5M2), hid_s[s][:]),
+                    False,
+                    s == 1,
+                )
 
         p_sb = [tile("p_sb%d" % h, [P, J], F32) for h in range(2)]
         pick = [[tile("pick%d_%d" % (h, i), [P, E], F32) for i in range(2)] for h in range(2)]

@@ -56,17 +56,17 @@ def tile_list_crossed_board_skip_bestoftwo_kernel(
         planes = tile("planes", [P, LATE + 3 * N], U8)
 
         nc.sync.dma_start(lists["o1"][:], offs)
-        nc.scalar.dma_start(out=xt_s[TOP:P, :].bitcast(I32), in_=xt_scales[0].bitcast(I32))
-        nc.sync.dma_start(lists["o2"][:], offs2)
-        nc.scalar.dma_start(out=xo_s[TOP:P, :].bitcast(I32), in_=xo_scales[0].bitcast(I32))
-        nc.sync.dma_start(out=xo_w[:].bitcast(I32), in_=words32(xo_words))
         nc.scalar.dma_start(out=wsc_raw[TOP:P, 0, :].bitcast(I32), in_=w_scales[0].bitcast(I32))
-        nc.sync.dma_start(out=w_raw[:].bitcast(I32), in_=words32(w_words))
+        nc.sync.dma_start(out=xt_s[TOP:P, :].bitcast(I32), in_=xt_scales[0].bitcast(I32))
         nc.scalar.dma_start(out=wsc_raw[TOP:P, 1, :].bitcast(I32), in_=w2_scales[0].bitcast(I32))
-        nc.sync.dma_start(out=w2_raw[:].bitcast(I32), in_=words32(w2_words))
-        nc.sync.dma_start(out=xt_w[:].bitcast(I32), in_=xt_words[0].bitcast(I32))
+        nc.sync.dma_start(lists["o2"][:], offs2)
+        nc.sync.dma_start(out=xo_s[TOP:P, :].bitcast(I32), in_=xo_scales[0].bitcast(I32))
+        nc.sync.dma_start(out=xo_w[:].bitcast(I32), in_=words32(xo_words))
+        nc.sync.dma_start(out=w_raw[:].bitcast(I32), in_=words32(w_words))
         nc.sync.dma_start(lists["o3"][:], offs3)
         nc.sync.dma_start(lists["o4"][:], offs4)
+        nc.sync.dma_start(out=w2_raw[:].bitcast(I32), in_=words32(w2_words))
+        nc.sync.dma_start(out=xt_w[:].bitcast(I32), in_=xt_words[0].bitcast(I32))
         nc.sync.dma_start(lists["o5"][:], offs5)
         nc.sync.dma_start(lists["o6"][:], offs6)
 
@@ -75,7 +75,7 @@ def tile_list_crossed_board_skip_bestoftwo_kernel(
         nc.vector.memset(wsc_raw[0:TOP, :, :].rearrange("p g r -> p (g r)").bitcast(I32), 0)
         boards = {t: tile("board%d" % t, [P, C], F32) for t in (0, 2)}
         for t in (0, 2):
-            nc.vector.memset(boards[t][:], 0.0)
+            nc.gpsimd.memset(boards[t][:], 0.0)
 
         xt_gs = tile("xt_gs", [P, J], U8)
         xo_gs = tile("xo_gs", [P, J], U8)
@@ -138,9 +138,8 @@ def tile_list_crossed_board_skip_bestoftwo_kernel(
             )
 
         a_sb = [tile("a_sb%d" % t, [P, J], F32) for t in range(PACK)]
-        a_ps = [ps.tile([P, J], F32, name="a_ps%d" % t) for t in range(PACK)]
+        a_ps = [ps.tile([P, J], F32, name="a_ps%d" % t, tag="bank%d" % t) for t in range(PACK)]
         b_ps = [ps.tile([P, 2, J], F32, name="b_ps%d" % u) for u in range(2)]
-        p_ps = [ps.tile([P, J], F32, name="p_ps%d" % h) for h in range(2)]
         H = J // 2
 
         def cols(op, lo, hi):
@@ -164,27 +163,35 @@ def tile_list_crossed_board_skip_bestoftwo_kernel(
         for t in range(PACK):
             mx(b_ps[t // 2][:, t % 2, :], w2_op(t), xt_op, True, False)
             mx(b_ps[t // 2][:, t % 2, :], w_op(t), xo_op, False, True)
-        for h in range(2):
-            mx(
-                p_ps[h][:],
-                (ws_w[:, P * h : P * (h + 1)].bitcast(E4M3), planes[:, LATE + 2 * N + P * h : LATE + 2 * N + P * (h + 1)]),
-                (sx_w[:].bitcast(E4M3), planes[:, LATE + N : LATE + 2 * N]),
-                True,
-                False,
-            )
+        p_tags = (("bank0", "bank2"), ("bank4", "bank5"))
+        p_ps = [[ps.tile([P, H], F32, name="p_ps%d_%d" % (s, h), tag=p_tags[s][h]) for h in range(2)] for s in range(2)]
+        for s in range(2):
+            for h in range(2):
+                mx(
+                    p_ps[s][h][:],
+                    (ws_w[:, P * h : P * (h + 1)].bitcast(E4M3), planes[:, LATE + 2 * N + P * h : LATE + 2 * N + P * (h + 1)]),
+                    cols((sx_w[:].bitcast(E4M3), planes[:, LATE + N : LATE + 2 * N]), H * s, H * (s + 1)),
+                    True,
+                    False,
+                )
 
-        read = [tile("read%d" % u, [P, 2, J], F32) for u in range(2)]
+        low = tile("low", [P, 2, J], F32)
+        high = [tile("high%d" % s, [P, 2, H], F32) for s in range(2)]
         for t in (0, 1):
-            nc.vector.tensor_copy(read[0][:, t, :], boards[t][:].indirect(lists["o4"][:]))
-        for t in (2, 3):
-            nc.scalar.activation(read[1][:, t - 2, :], boards[t][:].indirect(lists["o4"][:]), COPY)
+            nc.vector.tensor_copy(low[:, t, :], boards[t][:].indirect(lists["o4"][:]))
+        for s in range(2):
+            for t in (2, 3):
+                nc.scalar.activation(
+                    high[s][:, t - 2, :], boards[t][:].indirect(lists["o4"][:, 8 * s : 8 * (s + 1)]), COPY
+                )
+        read = [[low[:, :, 0:H], low[:, :, H:J]], [high[0][:], high[1][:]]]
 
         hid = [tile("hid%d" % s, [P, H, PACK], BF16) for s in range(2)]
         for u in range(2):
             for s in range(2):
                 nc.vector.tensor_tensor(
                     out=hid[s][:, :, 2 * u : 2 * u + 2],
-                    in0=read[u][:, :, H * s : H * (s + 1)].rearrange("p t j -> p j t"),
+                    in0=read[u][s].rearrange("p t j -> p j t"),
                     in1=b_ps[u][:, :, H * s : H * (s + 1)].rearrange("p t j -> p j t"),
                     op=MAX,
                 )
@@ -196,18 +203,20 @@ def tile_list_crossed_board_skip_bestoftwo_kernel(
             )
             for h in range(2):
                 mx(
-                    p_ps[h][:, H * s : H * (s + 1)],
+                    p_ps[s][h][:],
                     (wb_w[:, 2 * P * h : 2 * P * (h + 1)].bitcast(E2M1), planes[:, LATE + P * h : LATE + P * (h + 1)]),
                     (hid_w[s][:].bitcast(E5M2), hid_s[s][:]),
                     False,
-                    s == 1,
+                    True,
                 )
 
         p_sb = [tile("p_sb%d" % h, [P, J], F32) for h in range(2)]
         pick = [[tile("pick%d_%d" % (h, i), [P, E], F32) for i in range(2)] for h in range(2)]
         best = [tile("best%d" % h, [P, E], F32) for h in range(2)]
-        nc.vector.tensor_copy(out=p_sb[0][:], in_=p_ps[0][:])
-        nc.scalar.copy(out=p_sb[1][:], in_=p_ps[1][:])
+        for h in range(2):
+            nc.scalar.copy(out=p_sb[h][:, 0:H], in_=p_ps[0][h][:])
+        nc.vector.tensor_copy(out=p_sb[0][:, H:J], in_=p_ps[1][0][:])
+        nc.scalar.copy(out=p_sb[1][:, H:J], in_=p_ps[1][1][:])
         for i, name in enumerate(("o5", "o6")):
             nc.vector.tensor_copy(pick[0][i][:], p_sb[0][:].indirect(lists[name][:]))
             nc.scalar.activation(pick[1][i][:], p_sb[1][:].indirect(lists[name][:]), COPY)

@@ -16,9 +16,16 @@ MAX = mybir.AluOpType.max
 
 P = 128
 T, Z, J, R, C, N, E = 1024, 1024, 256, 512, 512, 256, 128
+H = J // 2
 PACK = 4
-ROWS = 16
-TOP = P - ROWS
+BLOCKS = 16
+TOP = P - BLOCKS
+PER_COLUMN = 16
+
+XT_AT, XO_AT, W_AT, W2_AT = 0, J, 2 * J, 2 * J + R
+FIRST_STAGE = 2 * J + 2 * R
+WB_AT, SX_AT, WS_AT = FIRST_STAGE, FIRST_STAGE + N, FIRST_STAGE + N + J
+SECOND_STAGE = 2 * N + J
 
 FLOPS = 2 * 512 * (4 * R * J + 2 * N * J)
 
@@ -40,9 +47,12 @@ def tile_list_crossed_board_skip_bestoftwo_kernel(
         def words32(dram):
             return dram[0].rearrange("p n t -> p (n t)").bitcast(I32)
 
+        def entries(name, lo, hi):
+            return lists[name][:, lo // PER_COLUMN : hi // PER_COLUMN]
+
         lists = {}
         for name, n in (("o1", J), ("o2", J), ("o3", J), ("o4", J), ("o5", E), ("o6", E)):
-            lists[name] = tile(name, [P, n // 16], U16)
+            lists[name] = tile(name, [P, n // PER_COLUMN], U16)
 
         xt_w = tile("xt_w", [P, T], U16)
         xo_w = early.tile([P, Z], U32, name="xo_w", offset=0, align_bytes=64)
@@ -51,16 +61,15 @@ def tile_list_crossed_board_skip_bestoftwo_kernel(
         w_raw = sb.tile([P, R], U32, name="w_raw", tag="raw_a", align_bytes=64)
         w2_raw = sb.tile([P, R], U32, name="w2_raw", tag="raw_b", align_bytes=64)
         wsc_raw = sb.tile([P, 2, R], U8, name="wsc_raw", tag="raw_c", align_bytes=64)
-        LATE = 2 * J + 2 * R
-        stage = tile("stage", [P, LATE], U8)
-        planes = tile("planes", [P, LATE + 3 * N], U8)
+        stage = tile("stage", [P, FIRST_STAGE], U8)
+        planes = tile("planes", [P, FIRST_STAGE + SECOND_STAGE], U8)
 
         nc.sync.dma_start(lists["o1"][:], offs)
         nc.scalar.dma_start(out=wsc_raw[TOP:P, 0, :].bitcast(I32), in_=w_scales[0].bitcast(I32))
         nc.sync.dma_start(out=xt_s[TOP:P, :].bitcast(I32), in_=xt_scales[0].bitcast(I32))
         nc.scalar.dma_start(out=wsc_raw[TOP:P, 1, :].bitcast(I32), in_=w2_scales[0].bitcast(I32))
         nc.sync.dma_start(lists["o2"][:], offs2)
-        nc.sync.dma_start(out=xo_s[TOP:P, :].bitcast(I32), in_=xo_scales[0].bitcast(I32))
+        nc.scalar.dma_start(out=xo_s[TOP:P, :].bitcast(I32), in_=xo_scales[0].bitcast(I32))
         nc.sync.dma_start(out=xo_w[:].bitcast(I32), in_=words32(xo_words))
         nc.sync.dma_start(out=w_raw[:].bitcast(I32), in_=words32(w_words))
         nc.sync.dma_start(lists["o3"][:], offs3)
@@ -82,11 +91,11 @@ def tile_list_crossed_board_skip_bestoftwo_kernel(
         nc.vector.tensor_copy(xt_gs[:], xt_s[:].indirect(lists["o1"][:]))
         nc.vector.tensor_copy(xo_gs[:], xo_s[:].indirect(lists["o2"][:]))
         nc.vector.tensor_copy(
-            out=stage[:, 2 * J : LATE].rearrange("p (g t m) -> p g t m", g=2, t=PACK),
+            out=stage[:, W_AT:FIRST_STAGE].rearrange("p (g t m) -> p g t m", g=2, t=PACK),
             in_=wsc_raw[:].rearrange("p g (m t) -> p g t m", t=PACK),
         )
-        nc.vector.tensor_copy(out=stage[:, 0:J].bitcast(I32), in_=xt_gs[:].bitcast(I32))
-        nc.vector.tensor_copy(out=stage[:, J : 2 * J].bitcast(I32), in_=xo_gs[:].bitcast(I32))
+        nc.vector.tensor_copy(out=stage[:, XT_AT : XT_AT + J].bitcast(I32), in_=xt_gs[:].bitcast(I32))
+        nc.vector.tensor_copy(out=stage[:, XO_AT : XO_AT + J].bitcast(I32), in_=xo_gs[:].bitcast(I32))
 
         def spread(first, width):
             for q in range(4):
@@ -95,24 +104,29 @@ def tile_list_crossed_board_skip_bestoftwo_kernel(
                     in_=stage[TOP + 4 * q : TOP + 4 * q + 4, 0:width].bitcast(I32),
                 )
 
-        spread(0, LATE)
-        for i, scales in enumerate((wb_scales, sx_scales, ws_scales)):
-            nc.sync.dma_start(out=stage[TOP:P, N * i : N * (i + 1)].bitcast(I32), in_=scales[0].bitcast(I32))
-        spread(LATE, 3 * N)
+        spread(0, FIRST_STAGE)
+        for scales, at in ((wb_scales, WB_AT), (sx_scales, SX_AT), (ws_scales, WS_AT)):
+            first = at - FIRST_STAGE
+            nc.sync.dma_start(
+                out=stage[TOP:P, first : first + scales.shape[2]].bitcast(I32), in_=scales[0].bitcast(I32)
+            )
+        spread(FIRST_STAGE, SECOND_STAGE)
 
         xt_g = tile("xt_g", [P, J], U16)
         xo_g = tile("xo_g", [P, J], U32)
         nc.vector.tensor_copy(xo_g[:], xo_w[:].indirect(lists["o2"][:]))
-        nc.vector.tensor_copy(xt_g[:], xt_w[:].indirect(lists["o1"][:]))
+        for lo in (0, H):
+            nc.vector.tensor_copy(xt_g[:, lo : lo + H], xt_w[:].indirect(entries("o1", lo, lo + H)))
         for t in (1, 3):
             boards[t] = early.tile([P, C], F32, name="board%d" % t, offset=4 * C * (t // 2), align_bytes=64)
             nc.vector.memset(boards[t][:], 0.0)
         w_p = tile("w_p", [P, R], U32)
         w2_p = tile("w2_p", [P, R], U32)
-        for dealt, raw in ((w_p, w_raw), (w2_p, w2_raw)):
+        every, even, odd = slice(0, PACK), slice(0, PACK, 2), slice(1, PACK, 2)
+        for dealt, raw, row_sets in ((w_p, w_raw, every), (w2_p, w2_raw, even), (w2_p, w2_raw, odd)):
             nc.scalar.copy(
-                out=dealt[:].rearrange("p (t m) -> p m t", t=PACK),
-                in_=raw[:].rearrange("p (m t) -> p m t", t=PACK),
+                out=dealt[:].rearrange("p (t m) -> p m t", t=PACK)[:, :, row_sets],
+                in_=raw[:].rearrange("p (m t) -> p m t", t=PACK)[:, :, row_sets],
             )
 
         sx_w = sb.tile([P, J], U32, name="sx_w", tag="raw_a", align_bytes=64)
@@ -122,15 +136,20 @@ def tile_list_crossed_board_skip_bestoftwo_kernel(
         nc.gpsimd.dma_start(out=ws_w[:].bitcast(I32), in_=words32(ws_words))
         nc.gpsimd.dma_start(out=wb_w[:].bitcast(I32), in_=wb_words[0].bitcast(I32))
 
-        xt_op = (xt_g[:].bitcast(E2M1), planes[:, 0:J])
-        xo_op = (xo_g[:].bitcast(E4M3), planes[:, J : 2 * J])
+        def operand(words, dtype, at, lo, hi):
+            return (words[:, lo:hi].bitcast(dtype), planes[:, at + lo : at + hi])
+
+        def xt_op(lo, hi):
+            return operand(xt_g, E2M1, XT_AT, lo, hi)
+
+        def xo_op(lo, hi):
+            return operand(xo_g, E4M3, XO_AT, lo, hi)
 
         def w_op(t):
-            return (w_p[:, P * t : P * (t + 1)].bitcast(E4M3), planes[:, 2 * J + P * t : 2 * J + P * (t + 1)])
+            return operand(w_p, E4M3, W_AT, P * t, P * (t + 1))
 
         def w2_op(t):
-            base = 2 * J + R
-            return (w2_p[:, P * t : P * (t + 1)].bitcast(E5M2), planes[:, base + P * t : base + P * (t + 1)])
+            return operand(w2_p, E5M2, W2_AT, P * t, P * (t + 1))
 
         def mx(dst, still, moving, start, stop):
             nc.tensor.matmul_mx(
@@ -140,13 +159,9 @@ def tile_list_crossed_board_skip_bestoftwo_kernel(
         a_sb = [tile("a_sb%d" % t, [P, J], F32) for t in range(PACK)]
         a_ps = [ps.tile([P, J], F32, name="a_ps%d" % t, tag="bank%d" % t) for t in range(PACK)]
         b_ps = [ps.tile([P, 2, J], F32, name="b_ps%d" % u) for u in range(2)]
-        H = J // 2
-
-        def cols(op, lo, hi):
-            return (op[0][:, lo:hi], op[1][:, lo:hi])
 
         def place(t, lo, hi):
-            where = boards[t][:].indirect(lists["o3"][:, lo // 16 : hi // 16])
+            where = boards[t][:].indirect(entries("o3", lo, hi))
             if t < 2:
                 nc.vector.tensor_copy(where, a_sb[t][:, lo:hi])
             else:
@@ -154,23 +169,24 @@ def tile_list_crossed_board_skip_bestoftwo_kernel(
 
         pieces = ((0, 0, H), (2, 0, H), (0, H, J), (2, H, J), (1, 0, J), (3, 0, J))
         for i, (t, lo, hi) in enumerate(pieces):
-            mx(a_ps[t][:, lo:hi], w_op(t), cols(xt_op, lo, hi), True, False)
-            mx(a_ps[t][:, lo:hi], w2_op(t), cols(xo_op, lo, hi), False, True)
+            mx(a_ps[t][:, lo:hi], w_op(t), xt_op(lo, hi), True, False)
+            mx(a_ps[t][:, lo:hi], w2_op(t), xo_op(lo, hi), False, True)
             nc.scalar.copy(out=a_sb[t][:, lo:hi], in_=a_ps[t][:, lo:hi])
             if i > 0:
                 place(*pieces[i - 1])
         place(*pieces[-1])
         for t in range(PACK):
-            mx(b_ps[t // 2][:, t % 2, :], w2_op(t), xt_op, True, False)
-            mx(b_ps[t // 2][:, t % 2, :], w_op(t), xo_op, False, True)
+            mx(b_ps[t // 2][:, t % 2, :], w2_op(t), xt_op(0, J), True, False)
+            mx(b_ps[t // 2][:, t % 2, :], w_op(t), xo_op(0, J), False, True)
+
         p_tags = (("bank0", "bank2"), ("bank4", "bank5"))
         p_ps = [[ps.tile([P, H], F32, name="p_ps%d_%d" % (s, h), tag=p_tags[s][h]) for h in range(2)] for s in range(2)]
         for s in range(2):
             for h in range(2):
                 mx(
                     p_ps[s][h][:],
-                    (ws_w[:, P * h : P * (h + 1)].bitcast(E4M3), planes[:, LATE + 2 * N + P * h : LATE + 2 * N + P * (h + 1)]),
-                    cols((sx_w[:].bitcast(E4M3), planes[:, LATE + N : LATE + 2 * N]), H * s, H * (s + 1)),
+                    operand(ws_w, E4M3, WS_AT, P * h, P * (h + 1)),
+                    operand(sx_w, E4M3, SX_AT, H * s, H * (s + 1)),
                     True,
                     False,
                 )
@@ -182,7 +198,7 @@ def tile_list_crossed_board_skip_bestoftwo_kernel(
         for s in range(2):
             for t in (2, 3):
                 nc.scalar.activation(
-                    high[s][:, t - 2, :], boards[t][:].indirect(lists["o4"][:, 8 * s : 8 * (s + 1)]), COPY
+                    high[s][:, t - 2, :], boards[t][:].indirect(entries("o4", H * s, H * (s + 1))), COPY
                 )
         read = [[low[:, :, 0:H], low[:, :, H:J]], [high[0][:], high[1][:]]]
 
@@ -204,7 +220,7 @@ def tile_list_crossed_board_skip_bestoftwo_kernel(
             for h in range(2):
                 mx(
                     p_ps[s][h][:],
-                    (wb_w[:, 2 * P * h : 2 * P * (h + 1)].bitcast(E2M1), planes[:, LATE + P * h : LATE + P * (h + 1)]),
+                    (wb_w[:, 2 * P * h : 2 * P * (h + 1)].bitcast(E2M1), planes[:, WB_AT + P * h : WB_AT + P * (h + 1)]),
                     (hid_w[s][:].bitcast(E5M2), hid_s[s][:]),
                     False,
                     True,

from contextlib import ExitStack

import concourse.mybir as mybir

F32 = mybir.dt.float32
BF16 = mybir.dt.bfloat16
I32 = mybir.dt.int32
U32 = mybir.dt.uint32
U16 = mybir.dt.uint16
U8 = mybir.dt.uint8
E4M3 = mybir.dt.float8_e4m3fn_x4
E5M2 = mybir.dt.float8_e5m2_x4
E2M1 = mybir.dt.float4_e2m1fn_x4
COPY = mybir.ActivationFunctionType.Copy
MAX = mybir.AluOpType.max

P = 128
T, Z, J, R, C, N, E = 1024, 1024, 256, 512, 512, 256, 128
H = J // 2
PACK = 4
BLOCKS = 16
TOP = P - BLOCKS
PER_COLUMN = 16

XT_AT, XO_AT, W_AT, W2_AT = 0, J, 2 * J, 2 * J + R
FIRST_STAGE = 2 * J + 2 * R
WB_AT, SX_AT, WS_AT = FIRST_STAGE, FIRST_STAGE + N, FIRST_STAGE + N + J
SECOND_STAGE = 2 * N + J

FLOPS = 2 * 512 * (4 * R * J + 2 * N * J)


def tile_list_crossed_board_skip_bestoftwo_kernel(
    tc, xt_words, xt_scales, xo_words, xo_scales, w_words, w_scales, w2_words, w2_scales,
    wb_words, wb_scales, sx_words, sx_scales, ws_words, ws_scales,
    offs, offs2, offs3, offs4, offs5, offs6, out,
):
    nc = tc.nc
    with ExitStack() as ctx:
        sb = ctx.enter_context(tc.tile_pool(name="sb", bufs=1))
        early = ctx.enter_context(tc.tile_pool(name="early", bufs=1))
        ps = ctx.enter_context(tc.psum_pool(name="ps", bufs=1))

        def tile(name, shape, dtype):
            return sb.tile(shape, dtype, name=name, align_bytes=64)

        def words32(dram):
            return dram[0].rearrange("p n t -> p (n t)").bitcast(I32)

        def entries(name, lo, hi):
            return lists[name][:, lo // PER_COLUMN : hi // PER_COLUMN]

        lists = {}
        for name, n in (("o1", J), ("o2", J), ("o3", J), ("o4", J), ("o5", E), ("o6", E)):
            lists[name] = tile(name, [P, n // PER_COLUMN], U16)

        xt_w = tile("xt_w", [P, T], U16)
        xo_w = early.tile([P, Z], U32, name="xo_w", offset=0, align_bytes=64)
        xt_s = tile("xt_s", [P, T], U8)
        xo_s = tile("xo_s", [P, Z], U8)
        w_raw = sb.tile([P, R], U32, name="w_raw", tag="raw_a", align_bytes=64)
        w2_raw = sb.tile([P, R], U32, name="w2_raw", tag="raw_b", align_bytes=64)
        wsc_raw = sb.tile([P, 2, R], U8, name="wsc_raw", tag="raw_c", align_bytes=64)
        stage = tile("stage", [P, FIRST_STAGE], U8)
        planes = tile("planes", [P, FIRST_STAGE + SECOND_STAGE], U8)

        nc.sync.dma_start(lists["o1"][:], offs)
        nc.scalar.dma_start(out=wsc_raw[TOP:P, 0, :].bitcast(I32), in_=w_scales[0].bitcast(I32))
        nc.sync.dma_start(out=xt_s[TOP:P, :].bitcast(I32), in_=xt_scales[0].bitcast(I32))
        nc.scalar.dma_start(out=wsc_raw[TOP:P, 1, :].bitcast(I32), in_=w2_scales[0].bitcast(I32))
        nc.sync.dma_start(lists["o2"][:], offs2)
        nc.scalar.dma_start(out=xo_s[TOP:P, :].bitcast(I32), in_=xo_scales[0].bitcast(I32))
        nc.sync.dma_start(out=xo_w[:].bitcast(I32), in_=words32(xo_words))
        nc.sync.dma_start(out=w_raw[:].bitcast(I32), in_=words32(w_words))
        nc.sync.dma_start(lists["o3"][:], offs3)
        nc.sync.dma_start(lists["o4"][:], offs4)
        nc.sync.dma_start(out=w2_raw[:].bitcast(I32), in_=words32(w2_words))
        nc.sync.dma_start(out=xt_w[:].bitcast(I32), in_=xt_words[0].bitcast(I32))
        nc.sync.dma_start(lists["o5"][:], offs5)
        nc.sync.dma_start(lists["o6"][:], offs6)

        nc.vector.memset(xt_s[0:TOP, :].bitcast(I32), 0)
        nc.vector.memset(xo_s[0:TOP, :].bitcast(I32), 0)
        nc.vector.memset(wsc_raw[0:TOP, :, :].rearrange("p g r -> p (g r)").bitcast(I32), 0)
        boards = {t: tile("board%d" % t, [P, C], F32) for t in (0, 2)}
        for t in (0, 2):
            nc.gpsimd.memset(boards[t][:], 0.0)

        xt_gs = tile("xt_gs", [P, J], U8)
        xo_gs = tile("xo_gs", [P, J], U8)
        nc.vector.tensor_copy(xt_gs[:], xt_s[:].indirect(lists["o1"][:]))
        nc.vector.tensor_copy(xo_gs[:], xo_s[:].indirect(lists["o2"][:]))
        nc.vector.tensor_copy(
            out=stage[:, W_AT:FIRST_STAGE].rearrange("p (g t m) -> p g t m", g=2, t=PACK),
            in_=wsc_raw[:].rearrange("p g (m t) -> p g t m", t=PACK),
        )
        nc.vector.tensor_copy(out=stage[:, XT_AT : XT_AT + J].bitcast(I32), in_=xt_gs[:].bitcast(I32))
        nc.vector.tensor_copy(out=stage[:, XO_AT : XO_AT + J].bitcast(I32), in_=xo_gs[:].bitcast(I32))

        def spread(first, width):
            for q in range(4):
                nc.sync.dma_start(
                    out=planes[32 * q : 32 * q + 4, first : first + width].bitcast(I32),
                    in_=stage[TOP + 4 * q : TOP + 4 * q + 4, 0:width].bitcast(I32),
                )

        spread(0, FIRST_STAGE)
        for scales, at in ((wb_scales, WB_AT), (sx_scales, SX_AT), (ws_scales, WS_AT)):
            first = at - FIRST_STAGE
            nc.sync.dma_start(
                out=stage[TOP:P, first : first + scales.shape[2]].bitcast(I32), in_=scales[0].bitcast(I32)
            )
        spread(FIRST_STAGE, SECOND_STAGE)

        xt_g = tile("xt_g", [P, J], U16)
        xo_g = tile("xo_g", [P, J], U32)
        nc.vector.tensor_copy(xo_g[:], xo_w[:].indirect(lists["o2"][:]))
        for lo in (0, H):
            nc.vector.tensor_copy(xt_g[:, lo : lo + H], xt_w[:].indirect(entries("o1", lo, lo + H)))
        for t in (1, 3):
            boards[t] = early.tile([P, C], F32, name="board%d" % t, offset=4 * C * (t // 2), align_bytes=64)
            nc.vector.memset(boards[t][:], 0.0)
        w_p = tile("w_p", [P, R], U32)
        w2_p = tile("w2_p", [P, R], U32)
        every, even, odd = slice(0, PACK), slice(0, PACK, 2), slice(1, PACK, 2)
        for dealt, raw, row_sets in ((w_p, w_raw, every), (w2_p, w2_raw, even), (w2_p, w2_raw, odd)):
            nc.scalar.copy(
                out=dealt[:].rearrange("p (t m) -> p m t", t=PACK)[:, :, row_sets],
                in_=raw[:].rearrange("p (m t) -> p m t", t=PACK)[:, :, row_sets],
            )

        sx_w = sb.tile([P, J], U32, name="sx_w", tag="raw_a", align_bytes=64)
        ws_w = sb.tile([P, N], U32, name="ws_w", tag="raw_b", align_bytes=64)
        wb_w = sb.tile([P, 2 * N], U8, name="wb_w", tag="raw_c", align_bytes=64)
        nc.gpsimd.dma_start(out=sx_w[:].bitcast(I32), in_=words32(sx_words))
        nc.gpsimd.dma_start(out=ws_w[:].bitcast(I32), in_=words32(ws_words))
        nc.gpsimd.dma_start(out=wb_w[:].bitcast(I32), in_=wb_words[0].bitcast(I32))

        def operand(words, dtype, at, lo, hi):
            return (words[:, lo:hi].bitcast(dtype), planes[:, at + lo : at + hi])

        def xt_op(lo, hi):
            return operand(xt_g, E2M1, XT_AT, lo, hi)

        def xo_op(lo, hi):
            return operand(xo_g, E4M3, XO_AT, lo, hi)

        def w_op(t):
            return operand(w_p, E4M3, W_AT, P * t, P * (t + 1))

        def w2_op(t):
            return operand(w2_p, E5M2, W2_AT, P * t, P * (t + 1))

        def mx(dst, still, moving, start, stop):
            nc.tensor.matmul_mx(
                out=dst, lhsT=still[0], lhsT_scale=still[1], rhs=moving[0], rhs_scale=moving[1], start=start, stop=stop
            )

        a_sb = [tile("a_sb%d" % t, [P, J], F32) for t in range(PACK)]
        a_ps = [ps.tile([P, J], F32, name="a_ps%d" % t, tag="bank%d" % t) for t in range(PACK)]
        b_ps = [ps.tile([P, 2, J], F32, name="b_ps%d" % u) for u in range(2)]

        def place(t, lo, hi):
            where = boards[t][:].indirect(entries("o3", lo, hi))
            if t < 2:
                nc.vector.tensor_copy(where, a_sb[t][:, lo:hi])
            else:
                nc.scalar.activation(where, a_sb[t][:, lo:hi], COPY)

        pieces = ((0, 0, H), (2, 0, H), (0, H, J), (2, H, J), (1, 0, J), (3, 0, J))
        for i, (t, lo, hi) in enumerate(pieces):
            mx(a_ps[t][:, lo:hi], w_op(t), xt_op(lo, hi), True, False)
            mx(a_ps[t][:, lo:hi], w2_op(t), xo_op(lo, hi), False, True)
            nc.scalar.copy(out=a_sb[t][:, lo:hi], in_=a_ps[t][:, lo:hi])
            if i > 0:
                place(*pieces[i - 1])
        place(*pieces[-1])
        for t in range(PACK):
            mx(b_ps[t // 2][:, t % 2, :], w2_op(t), xt_op(0, J), True, False)
            mx(b_ps[t // 2][:, t % 2, :], w_op(t), xo_op(0, J), False, True)

        p_tags = (("bank0", "bank2"), ("bank4", "bank5"))
        p_ps = [[ps.tile([P, H], F32, name="p_ps%d_%d" % (s, h), tag=p_tags[s][h]) for h in range(2)] for s in range(2)]
        for s in range(2):
            for h in range(2):
                mx(
                    p_ps[s][h][:],
                    operand(ws_w, E4M3, WS_AT, P * h, P * (h + 1)),
                    operand(sx_w, E4M3, SX_AT, H * s, H * (s + 1)),
                    True,
                    False,
                )

        low = tile("low", [P, 2, J], F32)
        high = [tile("high%d" % s, [P, 2, H], F32) for s in range(2)]
        for t in (0, 1):
            nc.vector.tensor_copy(low[:, t, :], boards[t][:].indirect(lists["o4"][:]))
        for s in range(2):
            for t in (2, 3):
                nc.scalar.activation(
                    high[s][:, t - 2, :], boards[t][:].indirect(entries("o4", H * s, H * (s + 1))), COPY
                )
        read = [[low[:, :, 0:H], low[:, :, H:J]], [high[0][:], high[1][:]]]

        hid = [tile("hid%d" % s, [P, H, PACK], BF16) for s in range(2)]
        for u in range(2):
            for s in range(2):
                nc.vector.tensor_tensor(
                    out=hid[s][:, :, 2 * u : 2 * u + 2],
                    in0=read[u][s].rearrange("p t j -> p j t"),
                    in1=b_ps[u][:, :, H * s : H * (s + 1)].rearrange("p t j -> p j t"),
                    op=MAX,
                )
        hid_w = [tile("hid_w%d" % s, [P, H], U32) for s in range(2)]
        hid_s = [tile("hid_s%d" % s, [P, H], U8) for s in range(2)]
        for s in range(2):
            nc.vector.quantize_mx(
                out=hid_w[s][:].bitcast(E5M2), scales=hid_s[s][:], in_=hid[s][:].rearrange("p j t -> p (j t)")
            )
            for h in range(2):
                mx(
                    p_ps[s][h][:],
                    (wb_w[:, 2 * P * h : 2 * P * (h + 1)].bitcast(E2M1), planes[:, WB_AT + P * h : WB_AT + P * (h + 1)]),
                    (hid_w[s][:].bitcast(E5M2), hid_s[s][:]),
                    False,
                    True,
                )

        p_sb = [tile("p_sb%d" % h, [P, J], F32) for h in range(2)]
        pick = [[tile("pick%d_%d" % (h, i), [P, E], F32) for i in range(2)] for h in range(2)]
        best = [tile("best%d" % h, [P, E], F32) for h in range(2)]
        for h in range(2):
            nc.scalar.copy(out=p_sb[h][:, 0:H], in_=p_ps[0][h][:])
        nc.vector.tensor_copy(out=p_sb[0][:, H:J], in_=p_ps[1][0][:])
        nc.scalar.copy(out=p_sb[1][:, H:J], in_=p_ps[1][1][:])
        for i, name in enumerate(("o5", "o6")):
            nc.vector.tensor_copy(pick[0][i][:], p_sb[0][:].indirect(lists[name][:]))
            nc.scalar.activation(pick[1][i][:], p_sb[1][:].indirect(lists[name][:]), COPY)
        for h in range(2):
            nc.vector.tensor_tensor(out=best[h][:], in0=pick[h][0][:], in1=pick[h][1][:], op=MAX)
            nc.sync.dma_start(out=out[P * h : P * (h + 1), :], in_=best[h][:])
